import numpy as np, ml_dtypes
CORES = [24,48,72,152,176,200]
N = 6
import mx_ref
NC = 512
WID = [148,512,128,406,254,216]
BF = ml_dtypes.bfloat16
def setup_inputs(rng):
    def f(*shape):
        return mx_ref.flush((rng.standard_normal(shape, dtype=np.float32) * np.exp2(rng.integers(-2, 3, shape[:-1] + (1,)))).astype(BF))
    return {"w": f(N, 128, 512), "x": f(N, 128, 4 * NC)}
def setup_inputs_blocks(rng):
    d = setup_inputs(rng)
    for k in ("w", "x"): d[k] = mx_ref.spread(d[k], rng, 4)
    return d
def setup_inputs_wide(rng):
    d = setup_inputs(rng)
    for k in ("w", "x"): d[k] = mx_ref.flush((d[k].astype(np.float32) * np.exp2(rng.integers(-8, 9, (N, 1, 1))).astype(np.float32)).astype(BF))
    return d
def setup_inputs_zeros(rng):
    d = setup_inputs(rng); v = d["x"].reshape(N, 128, -1, 4).copy()
    v[np.broadcast_to((rng.random((N, 1, v.shape[2], 1)) < 0.33), v.shape)] = 0
    d["x"] = v.reshape(d["x"].shape)
    return d
def reference(w, x):
    OFF = [sum(WID[:j]) for j in range(N + 1)]
    y = np.zeros((N, 128, OFF[N]), np.float32)
    for r in range(N):
        qw = mx_ref.quantize(w[r])
        for j in range(N):
            y[r][:, OFF[j]:OFF[j + 1]] = mx_ref.matmul(qw, mx_ref.quantize(x[j][:, :4 * WID[j]]))
    return {"y": y}

@@ -1,0 +1,211 @@
+from concourse.bass import DstId, RemoteDMATransfer
+from concourse.mybir import dt, ActivationFunctionType
+
+SLOT = 512
+NRANK = 6
+BANKS = 8
+MINW = 128
+
+SCRATCH = {
+    "xb": ("sbuf", [128, 4 * SLOT], "bfloat16"),
+    "wb": ("sbuf", [128, 512], "bfloat16"),
+    "qw": ("sbuf", [128, 128], "float8_e4m3fn_x4"),
+    "sw": ("sbuf", [128, 128], "uint8"),
+    "qx": ("sbuf", [128, NRANK * SLOT], "float8_e4m3fn_x4"),
+    "sx": ("sbuf", [128, NRANK * SLOT], "uint8"),
+    "yb": ("sbuf", [128, 1664], "float32"),
+    "ps": ("psum", [128, 512 * BANKS], "float32"),
+}
+SEMAPHORES = (["lx0", "lx1", "lw", "q0", "q1", "qw", "snt", "ts", "ta"]
+              + ["c%d" % k for k in range(BANKS)] + ["s%d" % k for k in range(BANKS)]
+              + ["m%d" % k for k in range(BANKS)] + ["p%d" % k for k in range(BANKS)])
+
+_CACHE = {}
+
+
+def _bits(mask):
+    return bin(mask).count("1")
+
+
+def _pieces(wid):
+    parts = [[(0, w)] for w in wid]
+    while sum(len(p) for p in parts) < BANKS:
+        best = None
+        for j, p in enumerate(parts):
+            for i, (a, b) in enumerate(p):
+                if b - a >= 2 * MINW and (best is None or b - a > best[0]):
+                    best = (b - a, j, i)
+        if best is None or len(parts[best[1]]) >= 2:
+            break
+        _, j, i = best
+        a, b = parts[j][i]
+        h = a + ((b - a) // 2 + 1) // 2 * 2
+        parts[j][i:i + 1] = [(a, h), (h, b)]
+    return [(j, a, b) for j, p in enumerate(parts) for (a, b) in p]
+
+
+def _plan(T, topo):
+    if "plan" in _CACHE:
+        return _CACHE["plan"]
+    cores = list(T.cores)
+    wid = list(T.tables["WID"])
+    n = len(cores)
+    pieces = _pieces(wid)
+    world = range((max(topo.host(c) for c in cores) + 1) * topo.CORES_PER_HOST)
+    ops, avail, tot, sent = {}, {}, {}, {}
+
+    def have(core, kind, a, b, sem):
+        avail.setdefault(core, []).append((kind, a, b, sem))
+
+    def emit(src, kind, a, b, dsts, sem):
+        mask = topo.mask(src, dsts[0])
+        for d in dsts:
+            mask &= topo.mask(src, d)
+        ops.setdefault(src, []).append((kind, a, b, tuple(dsts), sem, mask))
+        for d in dsts:
+            have(d, kind, a, b, sem)
+            tot.setdefault(d, {})
+            tot[d][sem] = tot[d].get(sem, 0) + _bits(mask)
+        sent[src] = sent.get(src, 0) + _bits(mask)
+
+    route = []
+    inflow = {}
+    for j, c in enumerate(cores):
+        others = [cores[(j + i) % n] for i in range(1, n)]
+        reach = [d for d in others if topo.may_write(c, d)]
+        far = [d for d in others if not topo.may_write(c, d)]
+        direct = reach[0]
+        rest = far + [d for d in reach if d != direct]
+        chip = [h for h in world if h != c and topo.host(h) == topo.host(c) and topo.chip(h) == topo.chip(c)]
+        ports = [h for h in chip if all(topo.may_write(h, d) for d in others)]
+        dies = sorted(set(topo.die(h) for h in ports), key=lambda x: x != topo.die(c))
+        route.append((direct, [rest[0::2], rest[1::2]], {x: [h for h in ports if topo.die(h) == x] for x in dies}, dies))
+        inflow[(direct, topo.die(c))] = inflow.get((direct, topo.die(c)), 0) + wid[j]
+    helpers = {}
+    for j in sorted(range(n), key=lambda j: -wid[j]):
+        direct, groups, side, dies = route[j]
+        jobs = [(k, gi) for k, p in enumerate(pieces) if p[0] == j for gi in range(2)]
+        best = None
+        for code in range(len(dies) ** len(jobs)):
+            pick = [dies[code // len(dies) ** i % len(dies)] for i in range(len(jobs))]
+            if any(pick.count(x) > len(side[x]) for x in dies):
+                continue
+            trial = dict(inflow)
+            for (k, gi), x in zip(jobs, pick):
+                for d in groups[gi]:
+                    trial[(d, x)] = trial.get((d, x), 0) + pieces[k][2] - pieces[k][1]
+            cost = (max(trial.values()), sum(v * v for v in trial.values()))
+            if best is None or cost < best[0]:
+                best = (cost, pick, trial)
+        inflow = best[2]
+        free = {x: list(side[x]) for x in dies}
+        for job, x in zip(jobs, best[1]):
+            helpers[job] = free[x].pop(0)
+
+    for j, c in enumerate(cores):
+        mine = [k for k, p in enumerate(pieces) if p[0] == j]
+        direct, groups = route[j][0], route[j][1]
+        tot.setdefault(c, {})
+        relay = []
+        for i, k in enumerate(mine):
+            a, b = SLOT * j + pieces[k][1], SLOT * j + pieces[k][2]
+            for kind in "cs":
+                have(c, kind, a, b, "q%d" % i)
+            tot[c]["q%d" % i] = 1
+            hs = [helpers[(k, gi)] for gi in range(2)]
+            emit(c, "c", a, b, hs, "c%d" % k)
+            emit(c, "s", a, b, hs, "s%d" % k)
+            relay += [(h, a, b, grp, k) for h, grp in zip(hs, groups)]
+        for h, a, b, grp, k in relay:
+            emit(h, "c", a, b, grp, "c%d" % k)
+            emit(h, "s", a, b, grp, "s%d" % k)
+        a, b = SLOT * j, SLOT * j + wid[j]
+        emit(c, "c", a, b, [direct], "c%d" % mine[0])
+        emit(c, "s", a, b, [direct], "s%d" % mine[0])
+
+    def waits(core, kinds, a, b):
+        sems = []
+        for kind, x, y, sem in avail.get(core, []):
+            if kind in kinds and x < b and a < y and sem not in sems:
+                sems.append(sem)
+        return [(s, tot[core][s]) for s in sems]
+
+    plan = {"pieces": pieces, "ops": ops, "waits": waits, "sent": sent, "wid": wid}
+    _CACHE["plan"] = plan
+    return plan
+
+
+def _send(g, T, topo, core, op):
+    kind, a, b, dsts, sem, mask = op
+    view = T.qx[:, a:b].bitcast(dt.uint8) if kind == "c" else T.sx[:, a:b]
+    ids = [topo.addr(d, core) for d in dsts]
+    if len(dsts) == 1:
+        g.remote_dma(view, view, T.sem[sem], T.sem.snt, ids[0][1], ids[0][0], mask)
+    else:
+        g.remote_dma_fused([RemoteDMATransfer(dst_ids=[DstId(rid=r, pnc=p) for r, p in ids], dma_engine_mask=mask,
+                                              remote_sem=T.sem[sem], srcs=[view], dsts=[view for _ in dsts])],
+                           local_sem=T.sem.snt)
+
+
+def rank_program(g, core, T, topo):
+    plan = _plan(T, topo)
+    S = T.sem
+    pieces, wid = plan["pieces"], plan["wid"]
+    r = T.rank_of(core)
+
+    if r is not None:
+        mine = [k for k, p in enumerate(pieces) if p[0] == r]
+        dmaq = [g.sync, g.scalar]
+        for i, k in enumerate(mine):
+            a, b = pieces[k][1], pieces[k][2]
+            dmaq[i % 2].dma_start(T.xb[:, 4 * a:4 * b], T.x[:, 4 * a:4 * b]).then_inc(S["lx%d" % i], 16)
+        dmaq[len(mine) % 2].dma_start(T.wb[:], T.w[:]).then_inc(S.lw, 16)
+        for i, k in enumerate(mine):
+            a, b = pieces[k][1], pieces[k][2]
+            g.vector.wait_ge(S["lx%d" % i], 16)
+            g.vector.quantize_mx(T.qx[:, SLOT * r + a:SLOT * r + b], T.sx[:, SLOT * r + a:SLOT * r + b],
+                                 T.xb[:, 4 * a:4 * b]).then_inc(S["q%d" % i], 1)
+        g.vector.wait_ge(S.lw, 16)
+        g.vector.quantize_mx(T.qw[:], T.sw[:], T.wb[:]).then_inc(S.qw, 1)
+
+    seen = {}
+    for op in plan["ops"].get(core, []):
+        for sem, cnt in plan["waits"](core, op[0], op[1], op[2]):
+            if seen.get(sem) != cnt:
+                g.wait_ge(S[sem], cnt)
+                seen[sem] = cnt
+        _send(g, T, topo, core, op)
+    if plan["sent"].get(core, 0):
+        g.wait_ge(S.snt, plan["sent"][core])
+
+    if r is None:
+        return
+
+    off = [sum(wid[:j]) for j in range(len(wid))]
+    order = mine + sorted([k for k in range(len(pieces)) if k not in mine], key=lambda k: (wid[pieces[k][0]], k))
+    g.tensor.wait_ge(S.qw, 1)
+    seen = {}
+    stores = [0, 0]
+    for pos, k in enumerate(order):
+        j, a, b = pieces[k]
+        ga, gb = SLOT * j + a, SLOT * j + b
+        for sem, cnt in plan["waits"](core, "cs", ga, gb):
+            if seen.get(sem) != cnt:
+                g.tensor.wait_ge(S[sem], cnt)
+                seen[sem] = cnt
+        acc = T.ps[:, 512 * k:512 * k + (b - a)]
+        out = T.yb[:, off[j] + a:off[j] + b]
+        g.tensor.matmul_mx(acc, T.qw[:], T.sw[:], T.qx[:, ga:gb], T.sx[:, ga:gb], True, True).then_inc(S["m%d" % k], 1)
+        if pos % 2 == 0:
+            g.vector.wait_ge(S["m%d" % k], 1)
+            g.vector.tensor_copy(out, acc).then_inc(S["p%d" % k], 1)
+            g.sync.wait_ge(S["p%d" % k], 1)
+            g.sync.dma_start(T.y[:, off[j] + a:off[j] + b], out).then_inc(S.ts, 16)
+        else:
+            g.scalar.wait_ge(S["m%d" % k], 1)
+            g.scalar.activation(out, acc, ActivationFunctionType.Copy).then_inc(S["p%d" % k], 1)
+            g.scalar.wait_ge(S["p%d" % k], 1)
+            g.scalar.dma_start(T.y[:, off[j] + a:off[j] + b], out).then_inc(S.ta, 16)
+        stores[pos % 2] += 16
+    g.sync.wait_ge(S.ts, stores[0])
+    g.scalar.wait_ge(S.ta, stores[1])

@@ -4,6 +4,7 @@ from concourse.mybir import dt, ActivationFunctionType
 SLOT = 512
 NRANK = 6
 BANKS = 8
+NCH = 12
 MINW = 128
 
 SCRATCH = {
@@ -16,8 +17,8 @@ SCRATCH = {
     "yb": ("sbuf", [128, 1664], "float32"),
     "ps": ("psum", [128, 512 * BANKS], "float32"),
 }
-SEMAPHORES = (["lx0", "lx1", "lw", "q0", "q1", "qw", "snt", "ts", "ta"]
-              + ["c%d" % k for k in range(BANKS)] + ["s%d" % k for k in range(BANKS)]
+SEMAPHORES = (["lx0", "lx1", "lx2", "lw", "q0", "q1", "q2", "qw", "snt", "ts", "ta"]
+              + ["c%d" % k for k in range(NCH)] + ["s%d" % k for k in range(NCH)]
               + ["m%d" % k for k in range(BANKS)] + ["p%d" % k for k in range(BANKS)])
 
 _CACHE = {}
@@ -27,21 +28,25 @@ def _bits(mask):
     return bin(mask).count("1")
 
 
-def _pieces(wid):
-    parts = [[(0, w)] for w in wid]
-    while sum(len(p) for p in parts) < BANKS:
-        best = None
-        for j, p in enumerate(parts):
-            for i, (a, b) in enumerate(p):
-                if b - a >= 2 * MINW and (best is None or b - a > best[0]):
-                    best = (b - a, j, i)
-        if best is None or len(parts[best[1]]) >= 2:
-            break
-        _, j, i = best
-        a, b = parts[j][i]
-        h = a + ((b - a) // 2 + 1) // 2 * 2
-        parts[j][i:i + 1] = [(a, h), (h, b)]
-    return [(j, a, b) for j, p in enumerate(parts) for (a, b) in p]
+def _chunks(wid):
+    out = []
+    for j, w in enumerate(wid):
+        if w >= 3 * MINW:
+            h = MINW + ((w - MINW) // 2 + 1) // 2 * 2
+            out += [(j, 0, MINW), (j, MINW, h), (j, h, w)]
+        else:
+            out.append((j, 0, w))
+    return out
+
+
+def _products(chunks, n):
+    out = []
+    for j in range(n):
+        mine = [c for c in chunks if c[0] == j]
+        if len(mine) > 1:
+            out.append((j, 0, mine[-1][1]))
+        out.append(mine[-1])
+    return out
 
 
 def _plan(T, topo):
@@ -50,15 +55,15 @@ def _plan(T, topo):
     cores = list(T.cores)
     wid = list(T.tables["WID"])
     n = len(cores)
-    pieces = _pieces(wid)
+    chunks = _chunks(wid)
     world = range((max(topo.host(c) for c in cores) + 1) * topo.CORES_PER_HOST)
     ops, avail, tot, sent = {}, {}, {}, {}
 
     def have(core, kind, a, b, sem):
         avail.setdefault(core, []).append((kind, a, b, sem))
 
-    def emit(src, kind, a, b, dsts, sem):
-        mask = topo.mask(src, dsts[0])
+    def emit(src, kind, a, b, dsts, sem, keep=-1):
+        mask = keep
         for d in dsts:
             mask &= topo.mask(src, d)
         ops.setdefault(src, []).append((kind, a, b, tuple(dsts), sem, mask))
@@ -69,7 +74,6 @@ def _plan(T, topo):
         sent[src] = sent.get(src, 0) + _bits(mask)
 
     route = []
-    inflow = {}
     for j, c in enumerate(cores):
         others = [cores[(j + i) % n] for i in range(1, n)]
         reach = [d for d in others if topo.may_write(c, d)]
@@ -79,46 +83,51 @@ def _plan(T, topo):
         chip = [h for h in world if h != c and topo.host(h) == topo.host(c) and topo.chip(h) == topo.chip(c)]
         ports = [h for h in chip if all(topo.may_write(h, d) for d in others)]
         dies = sorted(set(topo.die(h) for h in ports), key=lambda x: x != topo.die(c))
-        route.append((direct, [rest[0::2], rest[1::2]], {x: [h for h in ports if topo.die(h) == x] for x in dies}, dies))
-        inflow[(direct, topo.die(c))] = inflow.get((direct, topo.die(c)), 0) + wid[j]
-    helpers = {}
-    for j in sorted(range(n), key=lambda j: -wid[j]):
-        direct, groups, side, dies = route[j]
-        jobs = [(k, gi) for k, p in enumerate(pieces) if p[0] == j for gi in range(2)]
-        best = None
-        for code in range(len(dies) ** len(jobs)):
-            pick = [dies[code // len(dies) ** i % len(dies)] for i in range(len(jobs))]
-            if any(pick.count(x) > len(side[x]) for x in dies):
-                continue
-            trial = dict(inflow)
-            for (k, gi), x in zip(jobs, pick):
-                for d in groups[gi]:
-                    trial[(d, x)] = trial.get((d, x), 0) + pieces[k][2] - pieces[k][1]
-            cost = (max(trial.values()), sum(v * v for v in trial.values()))
-            if best is None or cost < best[0]:
-                best = (cost, pick, trial)
-        inflow = best[2]
-        free = {x: list(side[x]) for x in dies}
-        for job, x in zip(jobs, best[1]):
-            helpers[job] = free[x].pop(0)
+        side = [[h for h in ports if topo.die(h) == x] for x in dies]
+        route.append((direct, [rest[0::2], rest[1::2]], side, [k for k, p in enumerate(chunks) if p[0] == j]))
+
+    def pairs_of(j, flip):
+        side = route[j][2][::-1] if flip else route[j][2]
+        return [[side[0][0], side[1][0]], [side[1][1], side[0][1]]]
+
+    def jobs_of(j, flip):
+        pairs, mine = pairs_of(j, flip), route[j][3]
+        last = len(mine) - 1
+        jobs = []
+        for i, k in enumerate(mine):
+            jobs.append(("c", chunks[k][1], chunks[k][2], "c%d" % k, pairs[i % 2]))
+            if i == last - 1:
+                jobs.append(("s", 0, chunks[k][2], "s%d" % mine[0], pairs[(last + 1) % 2]))
+        jobs.append(("s", chunks[mine[last]][1], chunks[mine[last]][2], "s%d" % mine[last], pairs[(last + 1) % 2]))
+        return jobs
+
+    best = None
+    for code in range(2 ** n):
+        inflow = {}
+        for j, c in enumerate(cores):
+            key = (route[j][0], topo.die(c))
+            inflow[key] = inflow.get(key, 0) + 5 * wid[j]
+            for kind, a, b, _, pair in jobs_of(j, code >> j & 1):
+                for h, grp in zip(pair, route[j][1]):
+                    for d in grp:
+                        key = (d, topo.die(h))
+                        inflow[key] = inflow.get(key, 0) + (4 if kind == "c" else 1) * (b - a)
+        cost = (max(inflow.values()), sum(v * v for v in inflow.values()))
+        if best is None or cost < best[0]:
+            best = (cost, code)
 
     for j, c in enumerate(cores):
-        mine = [k for k, p in enumerate(pieces) if p[0] == j]
-        direct, groups = route[j][0], route[j][1]
+        direct, groups, _, mine = route[j]
+        home = ~topo.mask(c, direct)
         tot.setdefault(c, {})
-        relay = []
         for i, k in enumerate(mine):
-            a, b = SLOT * j + pieces[k][1], SLOT * j + pieces[k][2]
             for kind in "cs":
-                have(c, kind, a, b, "q%d" % i)
+                have(c, kind, SLOT * j + chunks[k][1], SLOT * j + chunks[k][2], "q%d" % i)
             tot[c]["q%d" % i] = 1
-            hs = [helpers[(k, gi)] for gi in range(2)]
-            emit(c, "c", a, b, hs, "c%d" % k)
-            emit(c, "s", a, b, hs, "s%d" % k)
-            relay += [(h, a, b, grp, k) for h, grp in zip(hs, groups)]
-        for h, a, b, grp, k in relay:
-            emit(h, "c", a, b, grp, "c%d" % k)
-            emit(h, "s", a, b, grp, "s%d" % k)
+        for kind, a, b, sem, pair in jobs_of(j, best[1] >> j & 1):
+            emit(c, kind, SLOT * j + a, SLOT * j + b, pair, sem, home)
+            for h, grp in zip(pair, groups):
+                emit(h, kind, SLOT * j + a, SLOT * j + b, grp, sem)
         a, b = SLOT * j, SLOT * j + wid[j]
         emit(c, "c", a, b, [direct], "c%d" % mine[0])
         emit(c, "s", a, b, [direct], "s%d" % mine[0])
@@ -130,7 +139,7 @@ def _plan(T, topo):
                 sems.append(sem)
         return [(s, tot[core][s]) for s in sems]
 
-    plan = {"pieces": pieces, "ops": ops, "waits": waits, "sent": sent, "wid": wid}
+    plan = {"chunks": chunks, "products": _products(chunks, n), "ops": ops, "waits": waits, "sent": sent, "wid": wid}
     _CACHE["plan"] = plan
     return plan
 
@@ -150,18 +159,16 @@ def _send(g, T, topo, core, op):
 def rank_program(g, core, T, topo):
     plan = _plan(T, topo)
     S = T.sem
-    pieces, wid = plan["pieces"], plan["wid"]
+    chunks, prods, wid = plan["chunks"], plan["products"], plan["wid"]
     r = T.rank_of(core)
 
     if r is not None:
-        mine = [k for k, p in enumerate(pieces) if p[0] == r]
+        mine = [p for p in chunks if p[0] == r]
         dmaq = [g.sync, g.scalar]
-        for i, k in enumerate(mine):
-            a, b = pieces[k][1], pieces[k][2]
+        for i, (_, a, b) in enumerate(mine):
             dmaq[i % 2].dma_start(T.xb[:, 4 * a:4 * b], T.x[:, 4 * a:4 * b]).then_inc(S["lx%d" % i], 16)
         dmaq[len(mine) % 2].dma_start(T.wb[:], T.w[:]).then_inc(S.lw, 16)
-        for i, k in enumerate(mine):
-            a, b = pieces[k][1], pieces[k][2]
+        for i, (_, a, b) in enumerate(mine):
             g.vector.wait_ge(S["lx%d" % i], 16)
             g.vector.quantize_mx(T.qx[:, SLOT * r + a:SLOT * r + b], T.sx[:, SLOT * r + a:SLOT * r + b],
                                  T.xb[:, 4 * a:4 * b]).then_inc(S["q%d" % i], 1)
@@ -182,12 +189,13 @@ def rank_program(g, core, T, topo):
         return
 
     off = [sum(wid[:j]) for j in range(len(wid))]
-    order = mine + sorted([k for k in range(len(pieces)) if k not in mine], key=lambda k: (wid[pieces[k][0]], k))
+    own = [k for k, p in enumerate(prods) if p[0] == r]
+    order = own + sorted([k for k in range(len(prods)) if k not in own], key=lambda k: (prods[k][2], k))
     g.tensor.wait_ge(S.qw, 1)
     seen = {}
     stores = [0, 0]
     for pos, k in enumerate(order):
-        j, a, b = pieces[k]
+        j, a, b = prods[k]
         ga, gb = SLOT * j + a, SLOT * j + b
         for sem, cnt in plan["waits"](core, "cs", ga, gb):
             if seen.get(sem) != cnt:

from concourse.bass import DstId, RemoteDMATransfer
from concourse.mybir import dt, ActivationFunctionType

SLOT = 512
NRANK = 6
BANKS = 8
NCH = 12
MINW = 128

SCRATCH = {
    "xb": ("sbuf", [128, 4 * SLOT], "bfloat16"),
    "wb": ("sbuf", [128, 512], "bfloat16"),
    "qw": ("sbuf", [128, 128], "float8_e4m3fn_x4"),
    "sw": ("sbuf", [128, 128], "uint8"),
    "qx": ("sbuf", [128, NRANK * SLOT], "float8_e4m3fn_x4"),
    "sx": ("sbuf", [128, NRANK * SLOT], "uint8"),
    "yb": ("sbuf", [128, 1664], "float32"),
    "ps": ("psum", [128, 512 * BANKS], "float32"),
}
SEMAPHORES = (["lx0", "lx1", "lx2", "lw", "q0", "q1", "q2", "qw", "snt", "ts", "ta"]
              + ["c%d" % k for k in range(NCH)] + ["s%d" % k for k in range(NCH)]
              + ["m%d" % k for k in range(BANKS)] + ["p%d" % k for k in range(BANKS)])

_CACHE = {}


def _bits(mask):
    return bin(mask).count("1")


def _chunks(wid):
    out = []
    for j, w in enumerate(wid):
        if w >= 3 * MINW:
            h = MINW + ((w - MINW) // 2 + 1) // 2 * 2
            out += [(j, 0, MINW), (j, MINW, h), (j, h, w)]
        else:
            out.append((j, 0, w))
    return out


def _products(chunks, n):
    out = []
    for j in range(n):
        mine = [c for c in chunks if c[0] == j]
        if len(mine) > 1:
            out.append((j, 0, mine[-1][1]))
        out.append(mine[-1])
    return out


def _plan(T, topo):
    if "plan" in _CACHE:
        return _CACHE["plan"]
    cores = list(T.cores)
    wid = list(T.tables["WID"])
    n = len(cores)
    chunks = _chunks(wid)
    world = range((max(topo.host(c) for c in cores) + 1) * topo.CORES_PER_HOST)
    ops, avail, tot, sent = {}, {}, {}, {}

    def have(core, kind, a, b, sem):
        avail.setdefault(core, []).append((kind, a, b, sem))

    def emit(src, kind, a, b, dsts, sem, keep=-1):
        mask = keep
        for d in dsts:
            mask &= topo.mask(src, d)
        ops.setdefault(src, []).append((kind, a, b, tuple(dsts), sem, mask))
        for d in dsts:
            have(d, kind, a, b, sem)
            tot.setdefault(d, {})
            tot[d][sem] = tot[d].get(sem, 0) + _bits(mask)
        sent[src] = sent.get(src, 0) + _bits(mask)

    route = []
    for j, c in enumerate(cores):
        others = [cores[(j + i) % n] for i in range(1, n)]
        reach = [d for d in others if topo.may_write(c, d)]
        far = [d for d in others if not topo.may_write(c, d)]
        direct = reach[0]
        rest = far + [d for d in reach if d != direct]
        chip = [h for h in world if h != c and topo.host(h) == topo.host(c) and topo.chip(h) == topo.chip(c)]
        ports = [h for h in chip if all(topo.may_write(h, d) for d in others)]
        dies = sorted(set(topo.die(h) for h in ports), key=lambda x: x != topo.die(c))
        side = [[h for h in ports if topo.die(h) == x] for x in dies]
        route.append((direct, [rest[0::2], rest[1::2]], side, [k for k, p in enumerate(chunks) if p[0] == j]))

    def pairs_of(j, flip):
        side = route[j][2][::-1] if flip else route[j][2]
        return [[side[0][0], side[1][0]], [side[1][1], side[0][1]]]

    def jobs_of(j, flip):
        pairs, mine = pairs_of(j, flip), route[j][3]
        last = len(mine) - 1
        jobs = []
        for i, k in enumerate(mine):
            jobs.append(("c", chunks[k][1], chunks[k][2], "c%d" % k, pairs[i % 2]))
            if i == last - 1:
                jobs.append(("s", 0, chunks[k][2], "s%d" % mine[0], pairs[(last + 1) % 2]))
        jobs.append(("s", chunks[mine[last]][1], chunks[mine[last]][2], "s%d" % mine[last], pairs[(last + 1) % 2]))
        return jobs

    best = None
    for code in range(2 ** n):
        inflow = {}
        for j, c in enumerate(cores):
            key = (route[j][0], topo.die(c))
            inflow[key] = inflow.get(key, 0) + 5 * wid[j]
            for kind, a, b, _, pair in jobs_of(j, code >> j & 1):
                for h, grp in zip(pair, route[j][1]):
                    for d in grp:
                        key = (d, topo.die(h))
                        inflow[key] = inflow.get(key, 0) + (4 if kind == "c" else 1) * (b - a)
        cost = (max(inflow.values()), sum(v * v for v in inflow.values()))
        if best is None or cost < best[0]:
            best = (cost, code)

    for j, c in enumerate(cores):
        direct, groups, _, mine = route[j]
        home = ~topo.mask(c, direct)
        tot.setdefault(c, {})
        for i, k in enumerate(mine):
            for kind in "cs":
                have(c, kind, SLOT * j + chunks[k][1], SLOT * j + chunks[k][2], "q%d" % i)
            tot[c]["q%d" % i] = 1
        for kind, a, b, sem, pair in jobs_of(j, best[1] >> j & 1):
            emit(c, kind, SLOT * j + a, SLOT * j + b, pair, sem, home)
            for h, grp in zip(pair, groups):
                emit(h, kind, SLOT * j + a, SLOT * j + b, grp, sem)
        a, b = SLOT * j, SLOT * j + wid[j]
        emit(c, "c", a, b, [direct], "c%d" % mine[0])
        emit(c, "s", a, b, [direct], "s%d" % mine[0])

    def waits(core, kinds, a, b):
        sems = []
        for kind, x, y, sem in avail.get(core, []):
            if kind in kinds and x < b and a < y and sem not in sems:
                sems.append(sem)
        return [(s, tot[core][s]) for s in sems]

    plan = {"chunks": chunks, "products": _products(chunks, n), "ops": ops, "waits": waits, "sent": sent, "wid": wid}
    _CACHE["plan"] = plan
    return plan


def _send(g, T, topo, core, op):
    kind, a, b, dsts, sem, mask = op
    view = T.qx[:, a:b].bitcast(dt.uint8) if kind == "c" else T.sx[:, a:b]
    ids = [topo.addr(d, core) for d in dsts]
    if len(dsts) == 1:
        g.remote_dma(view, view, T.sem[sem], T.sem.snt, ids[0][1], ids[0][0], mask)
    else:
        g.remote_dma_fused([RemoteDMATransfer(dst_ids=[DstId(rid=r, pnc=p) for r, p in ids], dma_engine_mask=mask,
                                              remote_sem=T.sem[sem], srcs=[view], dsts=[view for _ in dsts])],
                           local_sem=T.sem.snt)


def rank_program(g, core, T, topo):
    plan = _plan(T, topo)
    S = T.sem
    chunks, prods, wid = plan["chunks"], plan["products"], plan["wid"]
    r = T.rank_of(core)

    if r is not None:
        mine = [p for p in chunks if p[0] == r]
        dmaq = [g.sync, g.scalar]
        for i, (_, a, b) in enumerate(mine):
            dmaq[i % 2].dma_start(T.xb[:, 4 * a:4 * b], T.x[:, 4 * a:4 * b]).then_inc(S["lx%d" % i], 16)
        dmaq[len(mine) % 2].dma_start(T.wb[:], T.w[:]).then_inc(S.lw, 16)
        for i, (_, a, b) in enumerate(mine):
            g.vector.wait_ge(S["lx%d" % i], 16)
            g.vector.quantize_mx(T.qx[:, SLOT * r + a:SLOT * r + b], T.sx[:, SLOT * r + a:SLOT * r + b],
                                 T.xb[:, 4 * a:4 * b]).then_inc(S["q%d" % i], 1)
        g.vector.wait_ge(S.lw, 16)
        g.vector.quantize_mx(T.qw[:], T.sw[:], T.wb[:]).then_inc(S.qw, 1)

    seen = {}
    for op in plan["ops"].get(core, []):
        for sem, cnt in plan["waits"](core, op[0], op[1], op[2]):
            if seen.get(sem) != cnt:
                g.wait_ge(S[sem], cnt)
                seen[sem] = cnt
        _send(g, T, topo, core, op)
    if plan["sent"].get(core, 0):
        g.wait_ge(S.snt, plan["sent"][core])

    if r is None:
        return

    off = [sum(wid[:j]) for j in range(len(wid))]
    own = [k for k, p in enumerate(prods) if p[0] == r]
    order = own + sorted([k for k in range(len(prods)) if k not in own], key=lambda k: (prods[k][2], k))
    g.tensor.wait_ge(S.qw, 1)
    seen = {}
    stores = [0, 0]
    for pos, k in enumerate(order):
        j, a, b = prods[k]
        ga, gb = SLOT * j + a, SLOT * j + b
        for sem, cnt in plan["waits"](core, "cs", ga, gb):
            if seen.get(sem) != cnt:
                g.tensor.wait_ge(S[sem], cnt)
                seen[sem] = cnt
        acc = T.ps[:, 512 * k:512 * k + (b - a)]
        out = T.yb[:, off[j] + a:off[j] + b]
        g.tensor.matmul_mx(acc, T.qw[:], T.sw[:], T.qx[:, ga:gb], T.sx[:, ga:gb], True, True).then_inc(S["m%d" % k], 1)
        if pos % 2 == 0:
            g.vector.wait_ge(S["m%d" % k], 1)
            g.vector.tensor_copy(out, acc).then_inc(S["p%d" % k], 1)
            g.sync.wait_ge(S["p%d" % k], 1)
            g.sync.dma_start(T.y[:, off[j] + a:off[j] + b], out).then_inc(S.ts, 16)
        else:
            g.scalar.wait_ge(S["m%d" % k], 1)
            g.scalar.activation(out, acc, ActivationFunctionType.Copy).then_inc(S["p%d" % k], 1)
            g.scalar.wait_ge(S["p%d" % k], 1)
            g.scalar.dma_start(T.y[:, off[j] + a:off[j] + b], out).then_inc(S.ta, 16)
        stores[pos % 2] += 16
    g.sync.wait_ge(S.ts, stores[0])
    g.scalar.wait_ge(S.ta, stores[1])
